import numpy as np
CORES = [2,6,26,30,66,70,74,78,82,86]
N = 10
R, T, B = 8192, 2048, 256
def entries(a): return a.T.reshape(-1)
def pack(v, P): return np.ascontiguousarray(np.asarray(v, np.int32).reshape(-1, P).T)
def lists(rng, how):
    I = rng.integers(0, N * R, (N, T)); E = np.sort(rng.integers(0, T + 1, (N, B)), axis=1)
    if how == "void":
        E = np.zeros((N, B), np.int64)
        for r in range(N): k = np.sort(1 + rng.permutation(B - 2)[:6]); c = np.sort(1 + rng.permutation(T)[:6]); E[r] = np.concatenate([[0], c])[np.searchsorted(k, np.arange(B), side="right")]
        E[rng.integers(N)] = 0
    if how == "one":
        p = rng.permutation(N); z = rng.integers(0, B, N); z[p[0]] = 0; z[p[1]] = B - 1; E = np.where(np.arange(B)[None, :] < z[:, None], 0, T)
        I[p[::2]] = R * p[1] + I[p[::2]] % R
    if how == "single": E = np.broadcast_to(1 + np.arange(B), (N, B)).copy()
    if how == "hotrank": I = R * int(rng.integers(N)) + rng.integers(0, R, (N, T))
    if how == "edge": I = R * rng.integers(0, N, (N, T)) + np.where(rng.random((N, T)) < 0.5, 0, R - 1); E[:, -1] = T
    return {"idx": np.stack([pack(i, 16) for i in I]), "end": np.stack([pack(v, 16) for v in E])}
def setup_inputs(rng):
    return dict({"tab": rng.standard_normal((N, 128, R), dtype=np.float32)}, **lists(rng, "uniform"))
def setup_inputs_edge(rng):
    d = setup_inputs(rng); d.update(lists(rng, "edge"))
    for k in ("tab",): d[k] = (d[k].astype(np.float32) * 1048576.0).astype(d[k].dtype)
    return d
def setup_inputs_hotrank(rng):
    d = setup_inputs(rng); d.update(lists(rng, "hotrank"))
    for k in ("tab",): d[k] = (d[k].astype(np.float32) * (1 / 1024.0)).astype(d[k].dtype)
    return d
def setup_inputs_one(rng):
    d = setup_inputs(rng); d.update(lists(rng, "one"))
    return d
def setup_inputs_single(rng):
    d = setup_inputs(rng); d.update(lists(rng, "single"))
    return d
def setup_inputs_void(rng):
    d = setup_inputs(rng); d.update(lists(rng, "void"))
    return d
def check_inputs(x):
    bad = []
    if x["idx"].min() < 0 or x["idx"].max() >= N * R: bad.append("idx out of range")
    if x["end"].min() < 0 or x["end"].max() >= T + 1: bad.append("end out of range")
    if any((np.diff(entries(a)) < 0).any() for a in x["end"]): bad.append("end falls")
    t = x["tab"].astype(np.float32)
    if t.min() < -1e30 or t.max() > 1e30: bad.append("tab beyond -1e30 to 1e30")
    return bad
def reference(tab, idx, end):
    A = np.concatenate(list(tab), axis=1)
    y = np.zeros((N, 128, B), tab.dtype)
    for r in range(N):
        G = A[:, entries(idx[r])]; c = np.concatenate([[0], entries(end[r])])
        for b in range(B):
            if c[b + 1] > c[b]: y[r][:, b] = G[:, c[b]:c[b + 1]].max(axis=1)
    return {"y": y}

@@ -1,0 +1,372 @@
+from concourse.bass import DstId, RemoteDMATransfer
+from concourse.mybir import AluOpType, ActivationFunctionType
+
+N, R, L, B = 10, 8192, 2048, 256
+SIM = 96
+PAD = 4
+WIN = R + 2 * PAD
+MAXL = 6
+NG, NS, NLIM = 3, 2, 3
+H = L // 2
+LOAD = 1024
+PUSH = [1792, 1664, 1536, 1280, 1024, 896]
+BIGH = float(2 ** 99)
+NEV = 112
+
+SCRATCH = {
+    "win": ("sbuf", [128, WIN], "float32"),
+    "gat": ("sbuf", [128, NG * L], "float32"),
+    "sc0": ("sbuf", [128, L + PAD], "float32"),
+    "sc1": ("sbuf", [128, L + PAD], "float32"),
+    "res": ("sbuf", [128, MAXL * B], "float32"),
+    "land": ("sbuf", [128, N * B], "float32"),
+    "ysb": ("sbuf", [128, B], "float32"),
+    "limr": ("sbuf", [128, MAXL * L], "bfloat16"),
+    "bigr": ("sbuf", [128, 128], "bfloat16"),
+    "lx": ("sbuf", [128, MAXL * 128], "int32"),
+    "lf": ("sbuf", [128, MAXL * 128], "float32"),
+    "off": ("sbuf", [128, MAXL * 128], "uint16"),
+    "offp": ("sbuf", [128, MAXL * 16], "uint16"),
+    "seli": ("sbuf", [128, 128], "int32"),
+    "sel": ("sbuf", [128, 128], "float32"),
+    "io64": ("sbuf", [128, 64], "float32"),
+    "e1": ("sbuf", [128, 4], "int32"),
+    "eh": ("sbuf", [128, 4], "int32"),
+    "el": ("sbuf", [128, 4], "int32"),
+    "ehf": ("sbuf", [128, 4], "float32"),
+    "elf": ("sbuf", [128, 4], "float32"),
+    "ohh": ("sbuf", [128, 128], "bfloat16"),
+    "ohl": ("sbuf", [128, 64], "bfloat16"),
+    "limc": ("sbuf", [128, 32], "bfloat16"),
+    "e16": ("sbuf", [128, 16], "int32"),
+    "q16": ("sbuf", [128, 16], "int32"),
+    "pd": ("sbuf", [128, 16], "float32"),
+    "pn": ("sbuf", [128, 16], "float32"),
+    "pp": ("sbuf", [128, 16], "float32"),
+    "posu": ("sbuf", [128, 16], "uint16"),
+    "m1": ("dram", [128, 16], "int32"),
+    "m2": ("dram", [128, 16], "bfloat16"),
+    "m3": ("dram", [128, 16], "uint16"),
+    "l1": ("dram", [N, 128, 16], "int32"),
+    "l2": ("dram", [N, 128, 16], "bfloat16"),
+    "l3": ("dram", [N, 128, 16], "uint16"),
+    "lim0": ("psum", [128, H], "float32"),
+    "lim1": ("psum", [128, H], "float32"),
+    "lim2": ("psum", [128, H], "float32"),
+    "rp0": ("psum", [128, 512], "float32"),
+    "rp1": ("psum", [128, 512], "float32"),
+}
+SEMAPHORES = (["e%d" % k for k in range(NEV)] + ["i%d" % k for k in range(N)] + ["m%d" % k for k in range(N)]
+              + ["r%d" % k for k in range(N)] + ["w%d" % k for k in range(len(PUSH))] + ["loc"])
+
+
+def engines(mask):
+    return [b for b in range(16) if (mask >> b) & 1]
+
+
+def groups(topo, cores):
+    out = []
+    for o, c in enumerate(cores):
+        die = [x for x in range(SIM) if topo.chip(x) == topo.chip(c) and topo.die(x) == topo.die(c) and x != c]
+        able = [x for x in die if all(topo.may_write(x, d) for d in cores)]
+        rest = [x for x in die if x not in able[:1]]
+        h1, h2, h3 = able[0], rest[0], rest[1]
+        here = [q for q in range(N) if topo.chip(cores[q]) == topo.chip(c) and q != o]
+        offc = sorted([q for q in range(N) if topo.chip(cores[q]) != topo.chip(c)], key=lambda q: (q - o) % N)
+        near = [q for q in offc if topo.may_write(h2, cores[q])]
+        far = [q for q in offc if q not in near]
+        far.sort(key=lambda q: (not topo.mates(topo.chip(cores[q]), topo.chip(c)),
+                                topo.die(cores[q]) != topo.die(c), (q - o) % N))
+        near.sort(key=lambda q: (topo.die(cores[q]) != topo.die(c), (q - o) % N))
+        mine = far[:0:-1] + near[1:]
+        out.append([(c, mine), (h1, far[:1]), (h2, near[:1]), (h3, here + [o])])
+    return out
+
+
+def rank_program(g, core, T, topo):
+    cores = list(T.cores)
+    G = groups(topo, cores)
+    found = [(o, k) for o in range(N) for k in range(4) if G[o][k][0] == core]
+    if not found:
+        return
+    o, role = found[0]
+    lists = G[o][role][1]
+    n = len(lists)
+    isrank = role == 0
+    v, s, pe, sy = g.vector, g.scalar, g.tensor, g.sync
+    A = AluOpType
+    cnt = [0]
+    nloc = [0]
+
+    def ev(total=1):
+        e = (T.sem["e%d" % cnt[0]], total)
+        cnt[0] += 1
+        return e
+
+    def wait(q, *evs):
+        for e in evs:
+            q.wait_ge(e[0], e[1])
+
+    def handler(oo, q):
+        return [c for c, ls in G[oo] if q in ls][0]
+
+    def dst(x):
+        rid, pid, _ = topo.addr(x)
+        return DstId(rid=rid, pnc=pid)
+
+    e_off = [ev() for _ in lists]
+    e_lf = [ev() for _ in lists]
+    e_rp = [ev() for _ in lists]
+    e_lx = [ev(16) for _ in lists]
+    e_lr = [ev(32) for _ in lists]
+    e_g = [[ev(), ev()] for _ in lists]
+    e_lim = [[ev(2), ev(2)] for _ in lists]
+    e_sc = [[(e[0], 1), (e[0], 2)] for e in [ev() for _ in lists]]
+    e_ext = [ev() for _ in lists]
+    e_io, e_sel, e_m, e_sent, e_b0, e_big, e_pad = ev(), ev(), ev(2), ev(2), ev(), ev(), ev(2)
+    starts = [sum(PUSH[:k]) for k in range(len(PUSH))]
+    nload = R // LOAD
+    if isrank:
+        table = [ev(16) for _ in range(nload)]
+    else:
+        table = [(T.sem["w%d" % k], len(engines(topo.mask(cores[o], core)))) for k in range(len(PUSH))]
+
+    if isrank:
+        e_idx, e_e1, e_e16, e_z, e_q = ev(16), ev(16), ev(16), ev(), ev(32)
+        e_hl, e_hlf, e_oh, e_io64 = ev(2), ev(2), ev(4), ev()
+        e_cnt, e_limc, e_dn, e_pp, e_pr, e_posu = ev(), ev(), ev(2), ev(), ev(), ev()
+        e_m2, e_m3 = ev(16), ev(16)
+        s.dma_start(T.m1[:], T.idx[:]).then_inc(e_idx[0], 16)
+        s.dma_start(T.e1[:, 0:2], T.end[:]).then_inc(e_e1[0], 16)
+        s.dma_start(T.e16[0:16, :], T.end[:]).then_inc(e_e16[0], 16)
+        wait(s, e_z)
+        s.dma_start(T.q16[1:16, :], T.end[0:15, :]).then_inc(e_q[0], 16)
+        s.dma_start(T.q16[0:1, 1:16], T.end[15:16, 0:15]).then_inc(e_q[0], 16)
+        for k in range(nload):
+            if k >= 3:
+                wait(sy, table[k - 3])
+            sy.dma_start(T.win[:, PAD + k * LOAD:PAD + (k + 1) * LOAD],
+                         T.tab[:, k * LOAD:(k + 1) * LOAD]).then_inc(table[k][0], 16)
+
+    g.iota(T.seli[0:16, :], [[0, 8], [1, 16]], 0, -1).then_inc(e_io[0], 1)
+    if isrank:
+        v.memset(T.q16[0:16, :], 0).then_inc(e_z[0], 1)
+        g.iota(T.io64[:, :], [[1, 64]], 0, 0, allow_small_or_imprecise_dtypes=True).then_inc(e_io64[0], 1)
+    v.memset(T.bigr[0:1, :], BIGH).then_inc(e_b0[0], 1)
+    v.memset(T.win[:, 0:PAD], -BIGH).then_inc(e_m[0], 1)
+    v.memset(T.win[:, PAD + R:WIN], -BIGH).then_inc(e_m[0], 1)
+    v.memset(T.sc0[:, L:L + PAD], 0.0).then_inc(e_pad[0], 1)
+    v.memset(T.sc1[:, L:L + PAD], 0.0).then_inc(e_pad[0], 1)
+    wait(v, e_b0, e_m)
+    v.tensor_scalar(T.bigr[0:1, :], T.bigr[0:1, :], 2.0, None, A.mult).then_inc(e_big[0], 1)
+    v.tensor_scalar(T.win[:, 0:PAD], T.win[:, 0:PAD], 2.0, None, A.mult).then_inc(e_sent[0], 1)
+    v.tensor_scalar(T.win[:, PAD + R:WIN], T.win[:, PAD + R:WIN], 2.0, None, A.mult).then_inc(e_sent[0], 1)
+    wait(v, e_io)
+    v.tensor_scalar(T.sel[0:16, :], T.seli[0:16, :], 0.0, None, A.is_equal).then_inc(e_sel[0], 1)
+
+    if isrank:
+        wait(v, e_e1)
+        v.tensor_scalar(T.eh[:, 0:2], T.e1[:, 0:2], 5, None, A.arith_shift_right).then_inc(e_hl[0], 1)
+        v.tensor_scalar(T.el[:, 0:2], T.e1[:, 0:2], 31, None, A.bitwise_and).then_inc(e_hl[0], 1)
+        wait(v, e_e16, e_q)
+        v.tensor_scalar(T.pd[0:16, :], T.e16[0:16, :], float(-(L + 1)), None, A.add).then_inc(e_dn[0], 1)
+        v.tensor_tensor(T.pn[0:16, :], T.e16[0:16, :], T.q16[0:16, :], A.is_gt).then_inc(e_dn[0], 1)
+        wait(v, e_hl)
+        v.tensor_copy(T.ehf[:, 0:2], T.eh[:, 0:2]).then_inc(e_hlf[0], 1)
+        v.tensor_copy(T.elf[:, 0:2], T.el[:, 0:2]).then_inc(e_hlf[0], 1)
+        wait(v, e_dn)
+        v.tensor_tensor(T.pp[0:16, :], T.pd[0:16, :], T.pn[0:16, :], A.mult).then_inc(e_pp[0], 1)
+        wait(v, e_hlf, e_io64)
+        for k in range(2):
+            v.tensor_scalar(T.ohh[:, k * 64:(k + 1) * 64], T.io64[:, 0:64], T.ehf[:, k:k + 1], None,
+                            A.is_equal).then_inc(e_oh[0], 1)
+            v.tensor_scalar(T.ohl[:, k * 32:(k + 1) * 32], T.io64[:, 0:32], T.elf[:, k:k + 1], None,
+                            A.is_equal).then_inc(e_oh[0], 1)
+        wait(pe, e_sel, e_pp)
+        pe.matmul(T.rp1[:, 0:16], T.sel[0:16, :], T.pp[0:16, :], True, True).then_inc(e_pr[0], 1)
+        wait(pe, e_oh)
+        pe.matmul(T.rp0[0:64, 0:32], T.ohh[:, 0:64], T.ohl[:, 0:32], True, False)
+        pe.matmul(T.rp0[0:64, 0:32], T.ohh[:, 64:128], T.ohl[:, 32:64], False, True).then_inc(e_cnt[0], 1)
+        wait(v, e_pr)
+        v.tensor_scalar(T.posu[:, :], T.rp1[:, 0:16], float(L), None, A.add).then_inc(e_posu[0], 1)
+        wait(v, e_cnt)
+        v.tensor_scalar(T.limc[0:64, :], T.rp0[0:64, 0:32], -2.0, 1.0, A.mult, A.add).then_inc(e_limc[0], 1)
+        wait(s, e_posu)
+        s.dma_start(T.m3[:], T.posu[:, :]).then_inc(e_m3[0], 16)
+        wait(s, e_limc)
+        s.dma_start(T.m2[:], T.limc[0:64, :]).then_inc(e_m2[0], 16)
+
+        to = [handler(oo, o) for oo in range(N)]
+        m = topo.mask(core, to[0])
+        for x in to:
+            m &= topo.mask(core, x)
+        wait(g, e_idx)
+        g.remote_dma_fused([RemoteDMATransfer(
+            dst_ids=[dst(x) for x in to], dma_engine_mask=m, remote_sem=T.sem["i%d" % o],
+            srcs=[T.m1[:]], dsts=[T.l1[o] for _ in to])], local_sem=T.sem.loc)
+        es = engines(m)
+        half = [sum(1 << b for b in es[:len(es) // 2]), sum(1 << b for b in es[len(es) // 2:])]
+        wait(g, e_m3, e_m2)
+        g.remote_dma_fused([RemoteDMATransfer(
+            dst_ids=[dst(x) for x in to], dma_engine_mask=half[k], remote_sem=T.sem["m%d" % o],
+            srcs=[(T.m2, T.m3)[k][:]], dsts=[(T.l2, T.l3)[k][o] for _ in to]) for k in range(2)],
+            local_sem=T.sem.loc)
+        nloc[0] += 2 * len(es)
+    nmsg = len(engines(topo.mask(cores[0], cores[-1])))
+
+    lq = s if isrank else sy
+    for i, q in enumerate(lists):
+        lq.wait_ge(T.sem["i%d" % q], nmsg)
+        lq.dma_start(T.lx[0:16, i * 128:(i + 1) * 128], T.l1[q]).then_inc(e_lx[i][0], 16)
+    for i, q in enumerate(lists):
+        sy.wait_ge(T.sem["m%d" % q], nmsg)
+        sy.dma_start(T.limr[0:1, i * L:(i + 1) * L], T.l2[q]).then_inc(e_lr[i][0], 16)
+        sy.dma_start(T.offp[:, i * 16:(i + 1) * 16], T.l3[q]).then_inc(e_lr[i][0], 16)
+
+    RP = [T.rp0, T.rp1]
+
+    def offsets(i):
+        wait(v, e_rp[i])
+        v.tensor_copy(T.off[:, i * 128:(i + 1) * 128], RP[i % 2][:, 0:128]).then_inc(e_off[i][0], 1)
+
+    for i in range(n):
+        wait(v, e_lx[i])
+        v.tensor_scalar(T.lf[0:16, i * 128:(i + 1) * 128], T.lx[0:16, i * 128:(i + 1) * 128],
+                        float(PAD - R * o), float(R + PAD), A.add, A.min).then_inc(e_lf[i][0], 1)
+        if i:
+            offsets(i - 1)
+    offsets(n - 1)
+    wait(pe, e_sel)
+    if isrank:
+        wait(pe, e_posu, e_limc)
+    for i in range(n):
+        wait(pe, e_lf[i])
+        if i >= 2:
+            wait(pe, e_off[i - 2])
+        pe.matmul(RP[i % 2][:, 0:128], T.sel[0:16, :], T.lf[0:16, i * 128:(i + 1) * 128], True,
+                  True).then_inc(e_rp[i][0], 1)
+    LIM = [T.lim0, T.lim1, T.lim2]
+    wait(pe, e_big)
+    for i in range(n):
+        wait(pe, e_lr[i])
+        for h in range(2):
+            k = 2 * i + h
+            if k >= NLIM:
+                wait(pe, e_sc[(k - NLIM) // 2][(k - NLIM) % 2])
+            for b in range(2):
+                c0 = i * L + h * H + b * 512
+                pe.matmul(LIM[k % NLIM][:, b * 512:(b + 1) * 512], T.bigr[0:1, :], T.limr[0:1, c0:c0 + 512], True,
+                          True).then_inc(e_lim[i][h][0], 1)
+
+    SC = [T.sc0, T.sc1]
+
+    def window(i, h):
+        return (T.gat[:, (i % NG) * L + h * H:(i % NG) * L + (h + 1) * H],
+                T.win[:, 0:WIN].indirect(T.off[:, i * 128 + h * 64:i * 128 + (h + 1) * 64]))
+
+    def picked(i):
+        return T.res[:, i * B:(i + 1) * B], SC[i % NS][:, 0:L + PAD].indirect(T.offp[:, i * 16:(i + 1) * 16])
+
+    spick = (not isrank) and n == 2
+    wait(s, e_sent)
+    wait(s, *table)
+    for i in range(n):
+        wait(s, e_off[i])
+        if i >= NG:
+            wait(s, e_sc[i - NG][1])
+        for h in range(2):
+            if (i, h) != (0, 1):
+                a, b = window(i, h)
+                s.activation(a, b, ActivationFunctionType.Copy).then_inc(e_g[i][h][0], 1)
+    if spick:
+        wait(s, e_sc[0][1], e_lr[0], e_pad)
+        a, b = picked(0)
+        s.activation(a, b, ActivationFunctionType.Copy).then_inc(e_ext[0][0], 1)
+
+    wait(v, e_sent)
+    wait(v, *table)
+    wait(v, e_off[0], e_pad)
+    a, b = window(0, 1)
+    v.tensor_copy(a, b).then_inc(e_g[0][1][0], 1)
+    for i in range(n):
+        for h in range(2):
+            wait(v, e_g[i][h], e_lim[i][h])
+            if h == 0 and i >= NS:
+                wait(v, e_ext[i - NS])
+            if h == 1:
+                wait(v, e_sc[i][0])
+            ini = T.win[:, 0:1] if h == 0 else SC[i % NS][:, H - 1:H]
+            v.tensor_tensor_scan(SC[i % NS][:, h * H:(h + 1) * H], LIM[(2 * i + h) % NLIM][:, :],
+                                 T.gat[:, (i % NG) * L + h * H:(i % NG) * L + (h + 1) * H], ini, A.min,
+                                 A.max).then_inc(e_sc[i][h][0], 1)
+        if not (spick and i == 0):
+            wait(v, e_sc[i][1], e_lr[i])
+            a, b = picked(i)
+            v.tensor_copy(a, b).then_inc(e_ext[i][0], 1)
+
+    helpers = [G[o][k][0] for k in (1, 2, 3)]
+    if isrank:
+        got = 0
+        wait(g, table[nload - 3])
+        for k in range(len(PUSH)):
+            x = helpers[k % 3]
+            need = -(-(starts[k] + PUSH[k]) // LOAD)
+            for t in range(got, need):
+                if t != nload - 3:
+                    wait(g, table[t])
+            got = max(got, need)
+            blk = T.win[:, PAD + starts[k]:PAD + starts[k] + PUSH[k]]
+            rid, pid, _ = topo.addr(x)
+            mk = topo.mask(core, x)
+            g.remote_dma(blk, blk, T.sem["w%d" % k], T.sem.loc, pid, rid, mk)
+            nloc[0] += len(engines(mk))
+    else:
+        for k in range(len(PUSH)):
+            if helpers[k % 3] != core:
+                continue
+            wait(g, table[k])
+            blk = T.win[:, PAD + starts[k]:PAD + starts[k] + PUSH[k]]
+            others = [x for x in helpers if x != core]
+            mk = topo.mask(core, others[0])
+            g.remote_dma_fused([RemoteDMATransfer(
+                dst_ids=[dst(x) for x in others], dma_engine_mask=mk, remote_sem=T.sem["w%d" % k],
+                srcs=[blk], dsts=[blk for _ in others])], local_sem=T.sem.loc)
+            nloc[0] += len(engines(mk))
+
+    for i, q in enumerate(lists):
+        wait(g, e_ext[i])
+        x = cores[q]
+        rid, pid, _ = topo.addr(x)
+        mk = topo.mask(core, x)
+        g.remote_dma(T.land[:, o * B:(o + 1) * B], T.res[:, i * B:(i + 1) * B], T.sem["r%d" % o], T.sem.loc, pid, rid,
+                     mk)
+        nloc[0] += len(engines(mk))
+
+    if isrank:
+        order = []
+        for oo in range(N):
+            for role2, (c, ls) in enumerate(G[oo]):
+                if o in ls:
+                    p = ls.index(o)
+                    order.append(((p if role2 == 0 else 10 + 2 * p + (role2 < 3)), oo, c))
+        order.sort()
+        acc = T.rp0[:, 0:B]
+        prev = None
+        e_mx = ev()
+        for k, (_, oo, c) in enumerate(order):
+            v.wait_ge(T.sem["r%d" % oo], len(engines(topo.mask(c, core))))
+            if k == 0:
+                continue
+            if k == 1:
+                first = T.land[:, order[0][1] * B:(order[0][1] + 1) * B]
+            else:
+                wait(v, prev)
+                first = acc
+            prev = (e_mx[0], k)
+            v.tensor_tensor(T.ysb[:, :] if k == N - 1 else acc, first, T.land[:, oo * B:(oo + 1) * B],
+                            A.max).then_inc(prev[0], 1)
+        e_y = ev(16)
+        wait(sy, prev)
+        sy.dma_start(T.y[:], T.ysb[:, :]).then_inc(e_y[0], 16)
+        wait(sy, e_y)
+    g.wait_ge(T.sem.loc, nloc[0])

@@ -8,10 +8,12 @@ WIN = R + 2 * PAD
 MAXL = 6
 NG, NS, NLIM = 3, 2, 3
 H = L // 2
-LOAD = 1024
-PUSH = [1792, 1664, 1536, 1280, 1024, 896]
+LOADS = [(1024 * k, 1024) for k in range(8)]
+AHEAD = 3
+PUSH = [1792, 1600, 1408, 1152, 960, 768, 512]
+FLY = 2
 BIGH = float(2 ** 99)
-NEV = 112
+NEV = 104
 
 SCRATCH = {
     "win": ("sbuf", [128, WIN], "float32"),
@@ -57,7 +59,8 @@ SCRATCH = {
     "rp1": ("psum", [128, 512], "float32"),
 }
 SEMAPHORES = (["e%d" % k for k in range(NEV)] + ["i%d" % k for k in range(N)] + ["m%d" % k for k in range(N)]
-              + ["r%d" % k for k in range(N)] + ["w%d" % k for k in range(len(PUSH))] + ["loc"])
+              + ["r%d" % k for k in range(N)] + ["w%d" % k for k in range(len(PUSH))]
+              + ["p%d" % k for k in range(len(PUSH))] + ["loc"])
 
 
 def engines(mask):
@@ -125,9 +128,8 @@ def rank_program(g, core, T, topo):
     e_ext = [ev() for _ in lists]
     e_io, e_sel, e_m, e_sent, e_b0, e_big, e_pad = ev(), ev(), ev(2), ev(2), ev(), ev(), ev(2)
     starts = [sum(PUSH[:k]) for k in range(len(PUSH))]
-    nload = R // LOAD
     if isrank:
-        table = [ev(16) for _ in range(nload)]
+        table = [ev(16) for _ in LOADS]
     else:
         table = [(T.sem["w%d" % k], len(engines(topo.mask(cores[o], core)))) for k in range(len(PUSH))]
 
@@ -142,11 +144,10 @@ def rank_program(g, core, T, topo):
         wait(s, e_z)
         s.dma_start(T.q16[1:16, :], T.end[0:15, :]).then_inc(e_q[0], 16)
         s.dma_start(T.q16[0:1, 1:16], T.end[15:16, 0:15]).then_inc(e_q[0], 16)
-        for k in range(nload):
-            if k >= 3:
-                wait(sy, table[k - 3])
-            sy.dma_start(T.win[:, PAD + k * LOAD:PAD + (k + 1) * LOAD],
-                         T.tab[:, k * LOAD:(k + 1) * LOAD]).then_inc(table[k][0], 16)
+        for k, (c, w) in enumerate(LOADS):
+            if k >= AHEAD:
+                wait(sy, table[k - AHEAD])
+            sy.dma_start(T.win[:, PAD + c:PAD + c + w], T.tab[:, c:c + w]).then_inc(table[k][0], 16)
 
     g.iota(T.seli[0:16, :], [[0, 8], [1, 16]], 0, -1).then_inc(e_io[0], 1)
     if isrank:
@@ -305,33 +306,40 @@ def rank_program(g, core, T, topo):
             v.tensor_copy(a, b).then_inc(e_ext[i][0], 1)
 
     helpers = [G[o][k][0] for k in (1, 2, 3)]
+
+    def push(k, to, sem):
+        blk = T.win[:, PAD + starts[k]:PAD + starts[k] + PUSH[k]]
+        mk = topo.mask(core, to[0])
+        g.remote_dma_fused([RemoteDMATransfer(
+            dst_ids=[dst(x) for x in to], dma_engine_mask=mk, remote_sem=T.sem["w%d" % k],
+            srcs=[blk], dsts=[blk for _ in to])], local_sem=sem)
+        return len(engines(mk))
+
     if isrank:
-        got = 0
-        wait(g, table[nload - 3])
+        seen = []
+        out = []
+
+        def have(t):
+            if t not in seen:
+                seen.append(t)
+                wait(g, table[t])
+
+        have(len(LOADS) - 2)
         for k in range(len(PUSH)):
-            x = helpers[k % 3]
-            need = -(-(starts[k] + PUSH[k]) // LOAD)
-            for t in range(got, need):
-                if t != nload - 3:
-                    wait(g, table[t])
-            got = max(got, need)
-            blk = T.win[:, PAD + starts[k]:PAD + starts[k] + PUSH[k]]
-            rid, pid, _ = topo.addr(x)
-            mk = topo.mask(core, x)
-            g.remote_dma(blk, blk, T.sem["w%d" % k], T.sem.loc, pid, rid, mk)
-            nloc[0] += len(engines(mk))
+            for t in range(len(LOADS)):
+                if LOADS[t][0] < starts[k] + PUSH[k]:
+                    have(t)
+            if k >= FLY:
+                wait(g, out[k - FLY])
+            sem = T.sem["p%d" % k]
+            out.append((sem, push(k, [helpers[k % 3]], sem)))
+        last_out = out[-FLY:]
     else:
+        last_out = []
         for k in range(len(PUSH)):
-            if helpers[k % 3] != core:
-                continue
-            wait(g, table[k])
-            blk = T.win[:, PAD + starts[k]:PAD + starts[k] + PUSH[k]]
-            others = [x for x in helpers if x != core]
-            mk = topo.mask(core, others[0])
-            g.remote_dma_fused([RemoteDMATransfer(
-                dst_ids=[dst(x) for x in others], dma_engine_mask=mk, remote_sem=T.sem["w%d" % k],
-                srcs=[blk], dsts=[blk for _ in others])], local_sem=T.sem.loc)
-            nloc[0] += len(engines(mk))
+            if helpers[k % 3] == core:
+                wait(g, table[k])
+                nloc[0] += push(k, [x for x in helpers if x != core], T.sem.loc)
 
     for i, q in enumerate(lists):
         wait(g, e_ext[i])
@@ -369,4 +377,5 @@ def rank_program(g, core, T, topo):
         wait(sy, prev)
         sy.dma_start(T.y[:], T.ysb[:, :]).then_inc(e_y[0], 16)
         wait(sy, e_y)
+    wait(g, *last_out)
     g.wait_ge(T.sem.loc, nloc[0])

from concourse.bass import DstId, RemoteDMATransfer
from concourse.mybir import AluOpType, ActivationFunctionType

N, R, L, B = 10, 8192, 2048, 256
SIM = 96
PAD = 4
WIN = R + 2 * PAD
MAXL = 6
NG, NS, NLIM = 3, 2, 3
H = L // 2
LOADS = [(1024 * k, 1024) for k in range(8)]
AHEAD = 3
PUSH = [1792, 1600, 1408, 1152, 960, 768, 512]
FLY = 2
BIGH = float(2 ** 99)
NEV = 104

SCRATCH = {
    "win": ("sbuf", [128, WIN], "float32"),
    "gat": ("sbuf", [128, NG * L], "float32"),
    "sc0": ("sbuf", [128, L + PAD], "float32"),
    "sc1": ("sbuf", [128, L + PAD], "float32"),
    "res": ("sbuf", [128, MAXL * B], "float32"),
    "land": ("sbuf", [128, N * B], "float32"),
    "ysb": ("sbuf", [128, B], "float32"),
    "limr": ("sbuf", [128, MAXL * L], "bfloat16"),
    "bigr": ("sbuf", [128, 128], "bfloat16"),
    "lx": ("sbuf", [128, MAXL * 128], "int32"),
    "lf": ("sbuf", [128, MAXL * 128], "float32"),
    "off": ("sbuf", [128, MAXL * 128], "uint16"),
    "offp": ("sbuf", [128, MAXL * 16], "uint16"),
    "seli": ("sbuf", [128, 128], "int32"),
    "sel": ("sbuf", [128, 128], "float32"),
    "io64": ("sbuf", [128, 64], "float32"),
    "e1": ("sbuf", [128, 4], "int32"),
    "eh": ("sbuf", [128, 4], "int32"),
    "el": ("sbuf", [128, 4], "int32"),
    "ehf": ("sbuf", [128, 4], "float32"),
    "elf": ("sbuf", [128, 4], "float32"),
    "ohh": ("sbuf", [128, 128], "bfloat16"),
    "ohl": ("sbuf", [128, 64], "bfloat16"),
    "limc": ("sbuf", [128, 32], "bfloat16"),
    "e16": ("sbuf", [128, 16], "int32"),
    "q16": ("sbuf", [128, 16], "int32"),
    "pd": ("sbuf", [128, 16], "float32"),
    "pn": ("sbuf", [128, 16], "float32"),
    "pp": ("sbuf", [128, 16], "float32"),
    "posu": ("sbuf", [128, 16], "uint16"),
    "m1": ("dram", [128, 16], "int32"),
    "m2": ("dram", [128, 16], "bfloat16"),
    "m3": ("dram", [128, 16], "uint16"),
    "l1": ("dram", [N, 128, 16], "int32"),
    "l2": ("dram", [N, 128, 16], "bfloat16"),
    "l3": ("dram", [N, 128, 16], "uint16"),
    "lim0": ("psum", [128, H], "float32"),
    "lim1": ("psum", [128, H], "float32"),
    "lim2": ("psum", [128, H], "float32"),
    "rp0": ("psum", [128, 512], "float32"),
    "rp1": ("psum", [128, 512], "float32"),
}
SEMAPHORES = (["e%d" % k for k in range(NEV)] + ["i%d" % k for k in range(N)] + ["m%d" % k for k in range(N)]
              + ["r%d" % k for k in range(N)] + ["w%d" % k for k in range(len(PUSH))]
              + ["p%d" % k for k in range(len(PUSH))] + ["loc"])


def engines(mask):
    return [b for b in range(16) if (mask >> b) & 1]


def groups(topo, cores):
    out = []
    for o, c in enumerate(cores):
        die = [x for x in range(SIM) if topo.chip(x) == topo.chip(c) and topo.die(x) == topo.die(c) and x != c]
        able = [x for x in die if all(topo.may_write(x, d) for d in cores)]
        rest = [x for x in die if x not in able[:1]]
        h1, h2, h3 = able[0], rest[0], rest[1]
        here = [q for q in range(N) if topo.chip(cores[q]) == topo.chip(c) and q != o]
        offc = sorted([q for q in range(N) if topo.chip(cores[q]) != topo.chip(c)], key=lambda q: (q - o) % N)
        near = [q for q in offc if topo.may_write(h2, cores[q])]
        far = [q for q in offc if q not in near]
        far.sort(key=lambda q: (not topo.mates(topo.chip(cores[q]), topo.chip(c)),
                                topo.die(cores[q]) != topo.die(c), (q - o) % N))
        near.sort(key=lambda q: (topo.die(cores[q]) != topo.die(c), (q - o) % N))
        mine = far[:0:-1] + near[1:]
        out.append([(c, mine), (h1, far[:1]), (h2, near[:1]), (h3, here + [o])])
    return out


def rank_program(g, core, T, topo):
    cores = list(T.cores)
    G = groups(topo, cores)
    found = [(o, k) for o in range(N) for k in range(4) if G[o][k][0] == core]
    if not found:
        return
    o, role = found[0]
    lists = G[o][role][1]
    n = len(lists)
    isrank = role == 0
    v, s, pe, sy = g.vector, g.scalar, g.tensor, g.sync
    A = AluOpType
    cnt = [0]
    nloc = [0]

    def ev(total=1):
        e = (T.sem["e%d" % cnt[0]], total)
        cnt[0] += 1
        return e

    def wait(q, *evs):
        for e in evs:
            q.wait_ge(e[0], e[1])

    def handler(oo, q):
        return [c for c, ls in G[oo] if q in ls][0]

    def dst(x):
        rid, pid, _ = topo.addr(x)
        return DstId(rid=rid, pnc=pid)

    e_off = [ev() for _ in lists]
    e_lf = [ev() for _ in lists]
    e_rp = [ev() for _ in lists]
    e_lx = [ev(16) for _ in lists]
    e_lr = [ev(32) for _ in lists]
    e_g = [[ev(), ev()] for _ in lists]
    e_lim = [[ev(2), ev(2)] for _ in lists]
    e_sc = [[(e[0], 1), (e[0], 2)] for e in [ev() for _ in lists]]
    e_ext = [ev() for _ in lists]
    e_io, e_sel, e_m, e_sent, e_b0, e_big, e_pad = ev(), ev(), ev(2), ev(2), ev(), ev(), ev(2)
    starts = [sum(PUSH[:k]) for k in range(len(PUSH))]
    if isrank:
        table = [ev(16) for _ in LOADS]
    else:
        table = [(T.sem["w%d" % k], len(engines(topo.mask(cores[o], core)))) for k in range(len(PUSH))]

    if isrank:
        e_idx, e_e1, e_e16, e_z, e_q = ev(16), ev(16), ev(16), ev(), ev(32)
        e_hl, e_hlf, e_oh, e_io64 = ev(2), ev(2), ev(4), ev()
        e_cnt, e_limc, e_dn, e_pp, e_pr, e_posu = ev(), ev(), ev(2), ev(), ev(), ev()
        e_m2, e_m3 = ev(16), ev(16)
        s.dma_start(T.m1[:], T.idx[:]).then_inc(e_idx[0], 16)
        s.dma_start(T.e1[:, 0:2], T.end[:]).then_inc(e_e1[0], 16)
        s.dma_start(T.e16[0:16, :], T.end[:]).then_inc(e_e16[0], 16)
        wait(s, e_z)
        s.dma_start(T.q16[1:16, :], T.end[0:15, :]).then_inc(e_q[0], 16)
        s.dma_start(T.q16[0:1, 1:16], T.end[15:16, 0:15]).then_inc(e_q[0], 16)
        for k, (c, w) in enumerate(LOADS):
            if k >= AHEAD:
                wait(sy, table[k - AHEAD])
            sy.dma_start(T.win[:, PAD + c:PAD + c + w], T.tab[:, c:c + w]).then_inc(table[k][0], 16)

    g.iota(T.seli[0:16, :], [[0, 8], [1, 16]], 0, -1).then_inc(e_io[0], 1)
    if isrank:
        v.memset(T.q16[0:16, :], 0).then_inc(e_z[0], 1)
        g.iota(T.io64[:, :], [[1, 64]], 0, 0, allow_small_or_imprecise_dtypes=True).then_inc(e_io64[0], 1)
    v.memset(T.bigr[0:1, :], BIGH).then_inc(e_b0[0], 1)
    v.memset(T.win[:, 0:PAD], -BIGH).then_inc(e_m[0], 1)
    v.memset(T.win[:, PAD + R:WIN], -BIGH).then_inc(e_m[0], 1)
    v.memset(T.sc0[:, L:L + PAD], 0.0).then_inc(e_pad[0], 1)
    v.memset(T.sc1[:, L:L + PAD], 0.0).then_inc(e_pad[0], 1)
    wait(v, e_b0, e_m)
    v.tensor_scalar(T.bigr[0:1, :], T.bigr[0:1, :], 2.0, None, A.mult).then_inc(e_big[0], 1)
    v.tensor_scalar(T.win[:, 0:PAD], T.win[:, 0:PAD], 2.0, None, A.mult).then_inc(e_sent[0], 1)
    v.tensor_scalar(T.win[:, PAD + R:WIN], T.win[:, PAD + R:WIN], 2.0, None, A.mult).then_inc(e_sent[0], 1)
    wait(v, e_io)
    v.tensor_scalar(T.sel[0:16, :], T.seli[0:16, :], 0.0, None, A.is_equal).then_inc(e_sel[0], 1)

    if isrank:
        wait(v, e_e1)
        v.tensor_scalar(T.eh[:, 0:2], T.e1[:, 0:2], 5, None, A.arith_shift_right).then_inc(e_hl[0], 1)
        v.tensor_scalar(T.el[:, 0:2], T.e1[:, 0:2], 31, None, A.bitwise_and).then_inc(e_hl[0], 1)
        wait(v, e_e16, e_q)
        v.tensor_scalar(T.pd[0:16, :], T.e16[0:16, :], float(-(L + 1)), None, A.add).then_inc(e_dn[0], 1)
        v.tensor_tensor(T.pn[0:16, :], T.e16[0:16, :], T.q16[0:16, :], A.is_gt).then_inc(e_dn[0], 1)
        wait(v, e_hl)
        v.tensor_copy(T.ehf[:, 0:2], T.eh[:, 0:2]).then_inc(e_hlf[0], 1)
        v.tensor_copy(T.elf[:, 0:2], T.el[:, 0:2]).then_inc(e_hlf[0], 1)
        wait(v, e_dn)
        v.tensor_tensor(T.pp[0:16, :], T.pd[0:16, :], T.pn[0:16, :], A.mult).then_inc(e_pp[0], 1)
        wait(v, e_hlf, e_io64)
        for k in range(2):
            v.tensor_scalar(T.ohh[:, k * 64:(k + 1) * 64], T.io64[:, 0:64], T.ehf[:, k:k + 1], None,
                            A.is_equal).then_inc(e_oh[0], 1)
            v.tensor_scalar(T.ohl[:, k * 32:(k + 1) * 32], T.io64[:, 0:32], T.elf[:, k:k + 1], None,
                            A.is_equal).then_inc(e_oh[0], 1)
        wait(pe, e_sel, e_pp)
        pe.matmul(T.rp1[:, 0:16], T.sel[0:16, :], T.pp[0:16, :], True, True).then_inc(e_pr[0], 1)
        wait(pe, e_oh)
        pe.matmul(T.rp0[0:64, 0:32], T.ohh[:, 0:64], T.ohl[:, 0:32], True, False)
        pe.matmul(T.rp0[0:64, 0:32], T.ohh[:, 64:128], T.ohl[:, 32:64], False, True).then_inc(e_cnt[0], 1)
        wait(v, e_pr)
        v.tensor_scalar(T.posu[:, :], T.rp1[:, 0:16], float(L), None, A.add).then_inc(e_posu[0], 1)
        wait(v, e_cnt)
        v.tensor_scalar(T.limc[0:64, :], T.rp0[0:64, 0:32], -2.0, 1.0, A.mult, A.add).then_inc(e_limc[0], 1)
        wait(s, e_posu)
        s.dma_start(T.m3[:], T.posu[:, :]).then_inc(e_m3[0], 16)
        wait(s, e_limc)
        s.dma_start(T.m2[:], T.limc[0:64, :]).then_inc(e_m2[0], 16)

        to = [handler(oo, o) for oo in range(N)]
        m = topo.mask(core, to[0])
        for x in to:
            m &= topo.mask(core, x)
        wait(g, e_idx)
        g.remote_dma_fused([RemoteDMATransfer(
            dst_ids=[dst(x) for x in to], dma_engine_mask=m, remote_sem=T.sem["i%d" % o],
            srcs=[T.m1[:]], dsts=[T.l1[o] for _ in to])], local_sem=T.sem.loc)
        es = engines(m)
        half = [sum(1 << b for b in es[:len(es) // 2]), sum(1 << b for b in es[len(es) // 2:])]
        wait(g, e_m3, e_m2)
        g.remote_dma_fused([RemoteDMATransfer(
            dst_ids=[dst(x) for x in to], dma_engine_mask=half[k], remote_sem=T.sem["m%d" % o],
            srcs=[(T.m2, T.m3)[k][:]], dsts=[(T.l2, T.l3)[k][o] for _ in to]) for k in range(2)],
            local_sem=T.sem.loc)
        nloc[0] += 2 * len(es)
    nmsg = len(engines(topo.mask(cores[0], cores[-1])))

    lq = s if isrank else sy
    for i, q in enumerate(lists):
        lq.wait_ge(T.sem["i%d" % q], nmsg)
        lq.dma_start(T.lx[0:16, i * 128:(i + 1) * 128], T.l1[q]).then_inc(e_lx[i][0], 16)
    for i, q in enumerate(lists):
        sy.wait_ge(T.sem["m%d" % q], nmsg)
        sy.dma_start(T.limr[0:1, i * L:(i + 1) * L], T.l2[q]).then_inc(e_lr[i][0], 16)
        sy.dma_start(T.offp[:, i * 16:(i + 1) * 16], T.l3[q]).then_inc(e_lr[i][0], 16)

    RP = [T.rp0, T.rp1]

    def offsets(i):
        wait(v, e_rp[i])
        v.tensor_copy(T.off[:, i * 128:(i + 1) * 128], RP[i % 2][:, 0:128]).then_inc(e_off[i][0], 1)

    for i in range(n):
        wait(v, e_lx[i])
        v.tensor_scalar(T.lf[0:16, i * 128:(i + 1) * 128], T.lx[0:16, i * 128:(i + 1) * 128],
                        float(PAD - R * o), float(R + PAD), A.add, A.min).then_inc(e_lf[i][0], 1)
        if i:
            offsets(i - 1)
    offsets(n - 1)
    wait(pe, e_sel)
    if isrank:
        wait(pe, e_posu, e_limc)
    for i in range(n):
        wait(pe, e_lf[i])
        if i >= 2:
            wait(pe, e_off[i - 2])
        pe.matmul(RP[i % 2][:, 0:128], T.sel[0:16, :], T.lf[0:16, i * 128:(i + 1) * 128], True,
                  True).then_inc(e_rp[i][0], 1)
    LIM = [T.lim0, T.lim1, T.lim2]
    wait(pe, e_big)
    for i in range(n):
        wait(pe, e_lr[i])
        for h in range(2):
            k = 2 * i + h
            if k >= NLIM:
                wait(pe, e_sc[(k - NLIM) // 2][(k - NLIM) % 2])
            for b in range(2):
                c0 = i * L + h * H + b * 512
                pe.matmul(LIM[k % NLIM][:, b * 512:(b + 1) * 512], T.bigr[0:1, :], T.limr[0:1, c0:c0 + 512], True,
                          True).then_inc(e_lim[i][h][0], 1)

    SC = [T.sc0, T.sc1]

    def window(i, h):
        return (T.gat[:, (i % NG) * L + h * H:(i % NG) * L + (h + 1) * H],
                T.win[:, 0:WIN].indirect(T.off[:, i * 128 + h * 64:i * 128 + (h + 1) * 64]))

    def picked(i):
        return T.res[:, i * B:(i + 1) * B], SC[i % NS][:, 0:L + PAD].indirect(T.offp[:, i * 16:(i + 1) * 16])

    spick = (not isrank) and n == 2
    wait(s, e_sent)
    wait(s, *table)
    for i in range(n):
        wait(s, e_off[i])
        if i >= NG:
            wait(s, e_sc[i - NG][1])
        for h in range(2):
            if (i, h) != (0, 1):
                a, b = window(i, h)
                s.activation(a, b, ActivationFunctionType.Copy).then_inc(e_g[i][h][0], 1)
    if spick:
        wait(s, e_sc[0][1], e_lr[0], e_pad)
        a, b = picked(0)
        s.activation(a, b, ActivationFunctionType.Copy).then_inc(e_ext[0][0], 1)

    wait(v, e_sent)
    wait(v, *table)
    wait(v, e_off[0], e_pad)
    a, b = window(0, 1)
    v.tensor_copy(a, b).then_inc(e_g[0][1][0], 1)
    for i in range(n):
        for h in range(2):
            wait(v, e_g[i][h], e_lim[i][h])
            if h == 0 and i >= NS:
                wait(v, e_ext[i - NS])
            if h == 1:
                wait(v, e_sc[i][0])
            ini = T.win[:, 0:1] if h == 0 else SC[i % NS][:, H - 1:H]
            v.tensor_tensor_scan(SC[i % NS][:, h * H:(h + 1) * H], LIM[(2 * i + h) % NLIM][:, :],
                                 T.gat[:, (i % NG) * L + h * H:(i % NG) * L + (h + 1) * H], ini, A.min,
                                 A.max).then_inc(e_sc[i][h][0], 1)
        if not (spick and i == 0):
            wait(v, e_sc[i][1], e_lr[i])
            a, b = picked(i)
            v.tensor_copy(a, b).then_inc(e_ext[i][0], 1)

    helpers = [G[o][k][0] for k in (1, 2, 3)]

    def push(k, to, sem):
        blk = T.win[:, PAD + starts[k]:PAD + starts[k] + PUSH[k]]
        mk = topo.mask(core, to[0])
        g.remote_dma_fused([RemoteDMATransfer(
            dst_ids=[dst(x) for x in to], dma_engine_mask=mk, remote_sem=T.sem["w%d" % k],
            srcs=[blk], dsts=[blk for _ in to])], local_sem=sem)
        return len(engines(mk))

    if isrank:
        seen = []
        out = []

        def have(t):
            if t not in seen:
                seen.append(t)
                wait(g, table[t])

        have(len(LOADS) - 2)
        for k in range(len(PUSH)):
            for t in range(len(LOADS)):
                if LOADS[t][0] < starts[k] + PUSH[k]:
                    have(t)
            if k >= FLY:
                wait(g, out[k - FLY])
            sem = T.sem["p%d" % k]
            out.append((sem, push(k, [helpers[k % 3]], sem)))
        last_out = out[-FLY:]
    else:
        last_out = []
        for k in range(len(PUSH)):
            if helpers[k % 3] == core:
                wait(g, table[k])
                nloc[0] += push(k, [x for x in helpers if x != core], T.sem.loc)

    for i, q in enumerate(lists):
        wait(g, e_ext[i])
        x = cores[q]
        rid, pid, _ = topo.addr(x)
        mk = topo.mask(core, x)
        g.remote_dma(T.land[:, o * B:(o + 1) * B], T.res[:, i * B:(i + 1) * B], T.sem["r%d" % o], T.sem.loc, pid, rid,
                     mk)
        nloc[0] += len(engines(mk))

    if isrank:
        order = []
        for oo in range(N):
            for role2, (c, ls) in enumerate(G[oo]):
                if o in ls:
                    p = ls.index(o)
                    order.append(((p if role2 == 0 else 10 + 2 * p + (role2 < 3)), oo, c))
        order.sort()
        acc = T.rp0[:, 0:B]
        prev = None
        e_mx = ev()
        for k, (_, oo, c) in enumerate(order):
            v.wait_ge(T.sem["r%d" % oo], len(engines(topo.mask(c, core))))
            if k == 0:
                continue
            if k == 1:
                first = T.land[:, order[0][1] * B:(order[0][1] + 1) * B]
            else:
                wait(v, prev)
                first = acc
            prev = (e_mx[0], k)
            v.tensor_tensor(T.ysb[:, :] if k == N - 1 else acc, first, T.land[:, oo * B:(oo + 1) * B],
                            A.max).then_inc(prev[0], 1)
        e_y = ev(16)
        wait(sy, prev)
        sy.dma_start(T.y[:], T.ysb[:, :]).then_inc(e_y[0], 16)
        wait(sy, e_y)
    wait(g, *last_out)
    g.wait_ge(T.sem.loc, nloc[0])
